import numpy as np
CORES = [176,177,178,179,180,181,182,183,184,185,186,187,188,189,190,191,48,49,50,51,52,53,54,55,56,57,58,59,60,61,62,63]
N = 32
GROUPS = [[0,1,2,3,4,5,6,7],[8,9,10,11,12,13,14,15],[16,17,18,19,20,21,22,23],[24,25,26,27,28,29,30,31]]
def setup_inputs(rng):
    return {"x": rng.standard_normal((N, 128, 128), dtype=np.float32)}
def reference(x):
    y = np.empty((N, 128, 1024), x.dtype)
    for g in GROUPS:
        s = np.concatenate([x[r] for r in g], axis=1)
        for r in g:
            y[r] = s
    return {"y": y}

from concourse.bass import DstId, RemoteDMATransfer

W = 128
MEMBERS = 8
ENGINES = 16

SCRATCH = {
    "land": ("sbuf", [128, MEMBERS * W], "float32"),
}
SEMAPHORES = ["loaded", "arrived", "stored"]


def rank_program(g, core, T, topo):
    rank = T.rank_of(core)
    if rank is None:
        return

    group = [grp for grp in T.tables["GROUPS"] if rank in grp][0]
    j = group.index(rank)
    mine = T.land[:, j * W:(j + 1) * W]
    peers = [T.cores[r] for r in group if r != rank]

    g.sync.dma_start(mine, T.x[:]).then_inc(T.sem.loaded, ENGINES)

    g.wait_ge(T.sem.loaded, ENGINES)
    dst_ids = []
    for d in peers:
        rid, pid = topo.addr(d, core)
        dst_ids.append(DstId(rid=rid, pnc=pid))
    g.remote_dma_fused(
        [RemoteDMATransfer(
            dst_ids=dst_ids,
            dma_engine_mask=topo.mask(core, peers[0]),
            remote_sem=T.sem.arrived,
            srcs=[mine],
            dsts=[mine for d in peers],
            alu_op=0,
        )],
        local_sem=T.sem.arrived,
    )

    total = ENGINES * (len(peers) + 1)
    g.sync.wait_ge(T.sem.loaded, ENGINES)
    g.sync.wait_ge(T.sem.arrived, total)
    g.sync.dma_start(T.y[:], T.land[:]).then_inc(T.sem.stored, ENGINES)
    g.sync.wait_ge(T.sem.stored, ENGINES)

    g.wait_ge(T.sem.arrived, total)
    g.wait_ge(T.sem.stored, ENGINES)
